import numpy as np
import ml_dtypes


def mxq(x, axis, fmt="e4m3"):
    dtype, down = {"e4m3": (ml_dtypes.float8_e4m3fn, 7), "e5m2": (ml_dtypes.float8_e5m2, 14)}[fmt]
    v = np.moveaxis(np.asarray(x, np.float32).astype(ml_dtypes.bfloat16).astype(np.float64), axis, -1)
    blocks = v.reshape(v.shape[:-1] + (-1, 32))
    amax = np.abs(blocks).max(-1, keepdims=True)
    byte = np.maximum(np.where(amax > 0, np.frexp(amax)[1] - 1 + 127, 0) - down, 1)
    scale = np.exp2(byte - 127.0)
    codes = (blocks / scale).astype(np.float32).astype(dtype).astype(np.float64)
    return np.moveaxis((codes * scale).reshape(v.shape), -1, axis)


WIDE = False


def mx_kscale(k):
    if not WIDE:
        return np.ones(k)
    levels = np.array([10, -10, 5, -5, 0])
    if k % 512:
        return np.exp2(np.random.permutation(np.resize(levels, k // 32))).repeat(32)
    a = np.empty((k // 512, 16))
    for p in range(k // 512):
        a[p, :8] = np.random.permutation(np.resize(levels, 8))
        for g in range(8):
            far = levels[np.abs(levels - a[p, g]) >= 10]
            a[p, g + 8] = far[np.random.randint(len(far))]
    return np.exp2(a.ravel()).repeat(32)


def f64(x):
    return np.asarray(x).astype(np.float64)


def striped(idx):
    return np.tile(np.asarray(idx).reshape(-1, 16).T, (8, 1)).astype(np.uint16)


def unstriped(offs):
    return offs[:16].T.reshape(-1).astype(np.int64)


E2M1 = np.array([0.0, 0.5, 1.0, 1.5, 2.0, 3.0, 4.0, 6.0, -0.0, -0.5, -1.0, -1.5, -2.0, -3.0, -4.0, -6.0])


def pack_weight(w, fmt):
    k, n = w.shape
    w = f64(np.asarray(w, np.float32).astype(ml_dtypes.bfloat16)).reshape(k // 32, 32, n)
    amax = np.abs(w).max(1)
    if fmt == "e4m3":
        byte = np.frexp(amax)[1] - 1 + 127 - 7
    else:
        mant, ex = np.frexp(amax / 6.0)
        byte = np.where(mant > 0.5, ex, ex - 1) + 127
    byte = np.clip(np.where(amax > 0, byte, 1), 1, 254)
    scaled = (w * np.exp2(127.0 - byte)[:, None, :]).reshape(k, n).astype(np.float32)
    by_word = np.ascontiguousarray(scaled.reshape(k // 512, 128, 4, n).transpose(0, 1, 3, 2))
    if fmt == "e4m3":
        words = by_word.astype(ml_dtypes.float8_e4m3fn).view(np.uint8)
    else:
        c = by_word.astype(ml_dtypes.float4_e2m1fn).view(np.uint8) & 0xF
        words = (c[..., 0::2] | (c[..., 1::2] << 4)).reshape(k // 512, 128, 2 * n)
    return np.ascontiguousarray(words), np.ascontiguousarray(byte.astype(np.uint8).reshape(k // 512, 16, n))


def unpack_weight(words, scales, fmt):
    g, _, n = scales.shape
    words = np.ascontiguousarray(words).reshape(g, 128, n, -1)
    if fmt == "e4m3":
        vals = words.view(ml_dtypes.float8_e4m3fn).astype(np.float64)
    else:
        nib = np.empty((g, 128, n, 4), np.uint8)
        nib[..., 0::2] = words & 0xF
        nib[..., 1::2] = words >> 4
        vals = E2M1[nib]
    vals = vals * np.repeat(np.exp2(scales.astype(np.float64) - 127.0), 8, axis=1)[..., None]
    return vals.transpose(0, 1, 3, 2).reshape(g * 512, n)


def bf(x):
    return np.asarray(x, np.float32).astype(ml_dtypes.bfloat16)


def planes(Y):
    r, m = Y.shape
    b = f64(bf(Y)).reshape(r // 32, 32, m)
    amax = np.abs(b).max(1)
    byte = np.clip(np.where(amax > 0, np.frexp(amax)[1] - 1 + 127 - 7, 1), 1, 254)
    codes = (b * np.exp2(127.0 - byte)[:, None, :]).reshape(r, m).astype(np.float32).astype(ml_dtypes.float8_e4m3fn).view(np.uint8)
    words = codes.reshape(r // 512, 128, 4, m).transpose(0, 1, 3, 2)
    return np.ascontiguousarray(words), np.ascontiguousarray(byte.astype(np.uint8).reshape(r // 512, 16, m))


K, T, J, N = 1024, 2048, 512, 512


def setup_inputs():
    n = np.random.standard_normal
    idx = np.random.permutation(T)[:J]
    fk = mx_kscale(K)
    wap = pack_weight(n((K, N)) * 1 / np.sqrt(K) * fk[:, None], "e2m1")
    wbp = pack_weight(n((K, N)) * 1 / np.sqrt(K) * fk[:, None], "e4m3")
    return {
        "xq": (n((K, T)) / fk[:, None]).astype(np.float32),
        "wa_words": wap[0],
        "wa_scales": wap[1],
        "wb_words": wbp[0],
        "wb_scales": wbp[1],
        "offs": striped(idx),
    }


def reference(xq, wa_words, wa_scales, wb_words, wb_scales, offs):
    idx = unstriped(offs)
    wau = unpack_weight(wa_words, wa_scales, "e2m1")
    wbu = unpack_weight(wb_words, wb_scales, "e4m3")
    xqidxq = mxq(f64(xq)[:, idx], 0, "e4m3")
    p = wau.T @ xqidxq
    q = wbu.T @ xqidxq
    y = p + np.tanh(p - q)
    words, scales = planes(y)
    return y, words, scales

@@ -1,0 +1,215 @@
+from contextlib import ExitStack
+
+import concourse.mybir as mybir
+
+K, T, J, N = 1024, 2048, 512, 512
+FLOPS = 2 * 2 * K * N * J
+
+F32 = mybir.dt.float32
+BF16 = mybir.dt.bfloat16
+I32 = mybir.dt.int32
+U32 = mybir.dt.uint32
+U16 = mybir.dt.uint16
+U8 = mybir.dt.uint8
+FP8X4 = mybir.dt.float8_e4m3fn_x4
+FP4X4 = mybir.dt.float4_e2m1fn_x4
+ACT = mybir.ActivationFunctionType
+ALU = mybir.AluOpType
+
+P = 128
+PACK = 4
+PASSES = K // (P * PACK)
+CHUNK = 128
+CHUNKS = J // CHUNK
+LIST_COLS = CHUNK // 16
+QUADS = 4
+WB_ROW = 4
+ROWS_BEFORE_WEIGHTS = 6
+
+
+def tile_list_expert_contrast_pl_kernel(tc, xq, wa_words, wa_scales, wb_words, wb_scales, offs, out_0, out_1, out_2):
+    nc = tc.nc
+    with ExitStack() as ctx:
+        keep = ctx.enter_context(tc.tile_pool(name="keep", bufs=1))
+        psum = ctx.enter_context(tc.psum_pool(name="psum", bufs=1))
+
+        offsets = keep.tile([P, J // 16], U16, name="offsets")
+        x_rows = [keep.tile([P, T], F32, name="x_rows%d" % i) for i in range(PASSES * PACK)]
+        wa_raw = keep.tile([P, PASSES * 2 * N], U8, name="wa_raw", align_bytes=64)
+        wb_raw = keep.tile([P, PASSES * N], U32, name="wb_raw", align_bytes=64)
+        scale_raw = keep.tile([P, PASSES * N], U8, name="scale_raw", align_bytes=64)
+        xq_rows = xq.rearrange("(g p t) c -> g t p c", p=P, t=PACK)
+
+        def load_x(i):
+            nc.sync.dma_start(out=x_rows[i][:], in_=xq_rows[i // PACK, i % PACK])
+
+        load_x(0)
+        nc.sync.dma_start(offsets[:], offs)
+        for i in range(1, ROWS_BEFORE_WEIGHTS):
+            load_x(i)
+        nc.sync.dma_start(
+            out=wb_raw[:].bitcast(I32).rearrange("p (g n) -> p g n", g=PASSES),
+            in_=wb_words.rearrange("g p n t -> p g (n t)").bitcast(I32),
+        )
+        nc.sync.dma_start(
+            out=wa_raw[:].bitcast(I32).rearrange("p (g n) -> p g n", g=PASSES),
+            in_=wa_words.rearrange("g p n -> p g n").bitcast(I32),
+        )
+        for i in range(ROWS_BEFORE_WEIGHTS, PASSES * PACK):
+            load_x(i)
+
+        nc.gpsimd.memset(scale_raw[:].bitcast(I32), 0)
+        for scales, row in ((wa_scales, 0), (wb_scales, WB_ROW)):
+            for quad in range(QUADS):
+                first = 32 * quad + row
+                nc.gpsimd.dma_start(
+                    out=scale_raw[first : first + 4, :].bitcast(I32).rearrange("r (g n) -> r g n", g=PASSES),
+                    in_=scales[:, 4 * quad : 4 * quad + 4, :].rearrange("g r n -> r g n").bitcast(I32),
+                )
+
+        w_scale = keep.tile([P, PASSES * N], U8, name="w_scale", align_bytes=64)
+
+        x_codes = {}
+        x_scale = {}
+
+        def quantise_x(g, first, count, woven):
+            codes = keep.tile([P, count * CHUNK], U32, name="x_codes%d_%d" % (g, first), align_bytes=64)
+            scale = keep.tile([P, count * CHUNK], U8, name="x_scale%d_%d" % (g, first), align_bytes=64)
+            nc.vector.quantize_mx(out=codes[:].bitcast(FP8X4), scales=scale[:], in_=woven[:].rearrange("p j t -> p (j t)"))
+            for c in range(count):
+                x_codes[g, first + c] = codes[:, c * CHUNK : (c + 1) * CHUNK]
+                x_scale[g, first + c] = scale[:, c * CHUNK : (c + 1) * CHUNK]
+
+        def listed(c, count):
+            return offsets[:, c * LIST_COLS : (c + count) * LIST_COLS]
+
+        wa_dealt = [keep.tile([P, 2 * N], U8, name="wa_dealt%d" % g, align_bytes=64) for g in range(PASSES)]
+        wb_dealt = [keep.tile([P, N], U32, name="wb_dealt%d" % g, align_bytes=64) for g in range(PASSES)]
+
+        def deal_weights(g):
+            nc.vector.tensor_copy(
+                out=wb_dealt[g][:].rearrange("p (t m) -> p m t", t=PACK),
+                in_=wb_raw[:, g * N : (g + 1) * N].rearrange("p (m t) -> p m t", t=PACK),
+            )
+            nc.scalar.copy(
+                out=wa_dealt[g][:].bitcast(U16).rearrange("p (t m) -> p m t", t=PACK),
+                in_=wa_raw[:, g * 2 * N : (g + 1) * 2 * N].bitcast(U16).rearrange("p (m t) -> p m t", t=PACK),
+            )
+
+        p_bank = [psum.tile([P, PACK * CHUNK], F32, name="p_bank%d" % c) for c in range(CHUNKS)]
+        q_bank = [psum.tile([P, PACK * CHUNK], F32, name="q_bank%d" % c) for c in range(CHUNKS)]
+
+        def multiply(g, c):
+            for t in range(PACK):
+                cols = slice(g * N + t * P, g * N + (t + 1) * P)
+                nc.tensor.matmul_mx(
+                    out=q_bank[c][:, t * CHUNK : (t + 1) * CHUNK],
+                    lhsT=wb_dealt[g][:, t * P : (t + 1) * P].bitcast(FP8X4),
+                    lhsT_scale=w_scale[WB_ROW:P, cols],
+                    rhs=x_codes[g, c].bitcast(FP8X4),
+                    rhs_scale=x_scale[g, c],
+                    start=(g == 0 and t == 0),
+                    stop=(g == PASSES - 1 and t == PACK - 1),
+                )
+            for t in range(PACK):
+                cols = slice(g * N + t * P, g * N + (t + 1) * P)
+                nc.tensor.matmul_mx(
+                    out=p_bank[c][:, t * CHUNK : (t + 1) * CHUNK],
+                    lhsT=wa_dealt[g][:, t * 2 * P : (t + 1) * 2 * P].bitcast(FP4X4),
+                    lhsT_scale=w_scale[:, cols],
+                    rhs=x_codes[g, c].bitcast(FP8X4),
+                    rhs_scale=x_scale[g, c],
+                    start=(g == 0 and t == 0),
+                    stop=(g == PASSES - 1 and t == PACK - 1),
+                )
+
+        outer = (0, CHUNKS - 1)
+        for g in range(PASSES):
+            inner_woven = keep.tile([P, 2 * CHUNK, PACK], BF16, name="inner_woven%d" % g, align_bytes=64)
+            picked = {c: keep.tile([P, PACK, CHUNK], BF16, name="picked%d_%d" % (g, c)) for c in outer}
+            woven = {c: keep.tile([P, CHUNK, PACK], BF16, name="woven%d_%d" % (g, c), align_bytes=64) for c in outer}
+            for t in range(PACK):
+                window = x_rows[g * PACK + t]
+                if g * PACK + t == ROWS_BEFORE_WEIGHTS:
+                    nc.vector.tensor_copy(
+                        out=w_scale[:].rearrange("p (g t m) -> p g m t", g=PASSES, t=PACK),
+                        in_=scale_raw[:].rearrange("p (g m t) -> p g m t", g=PASSES, t=PACK),
+                    )
+                    for h in range(PASSES):
+                        deal_weights(h)
+                    for c in range(CHUNKS):
+                        multiply(0, c)
+                nc.vector.tensor_copy(out=inner_woven[:, :, t], in_=window[:].indirect(listed(1, 2)))
+                for c in outer:
+                    nc.scalar.activation(out=picked[c][:, t, :], in_=window[:].indirect(listed(c, 1)), func=ACT.Copy)
+                    if t >= PACK - 2:
+                        rows = slice(0, PACK - 1) if t == PACK - 2 else slice(t, PACK)
+                        nc.scalar.copy(out=woven[c][:, :, rows], in_=picked[c][:, rows, :].rearrange("p t j -> p j t"))
+            quantise_x(g, outer[0], 1, woven[outer[0]])
+            quantise_x(g, 1, 2, inner_woven)
+            quantise_x(g, outer[1], 1, woven[outer[1]])
+
+        for c in range(CHUNKS):
+            multiply(PASSES - 1, c)
+
+        y_rows = out_0.rearrange("(p t) j -> p t j", t=PACK)
+        words = out_1[0].rearrange("p j t -> p (j t)").bitcast(I32)
+        y_scale = keep.tile([P, J], U8, name="y_scale", align_bytes=64)
+        q_sb = [keep.tile([P, PACK * CHUNK], F32, name="q_sb%d" % c) for c in range(CHUNKS)]
+        diff = [keep.tile([P, PACK * CHUNK], F32, name="diff%d" % c) for c in range(CHUNKS)]
+        bent = [keep.tile([P, PACK * CHUNK], F32, name="bent%d" % c) for c in range(CHUNKS)]
+        y = [keep.tile([P, PACK, CHUNK], F32, name="y%d" % c) for c in range(CHUNKS)]
+        last = CHUNKS - 1
+        early_woven = keep.tile([P, last * CHUNK, PACK], BF16, name="early_woven", align_bytes=64)
+        last_woven = keep.tile([P, CHUNK, PACK], BF16, name="last_woven", align_bytes=64)
+
+        def fetch_q(c):
+            nc.scalar.copy(out=q_sb[c][:], in_=q_bank[c][:])
+
+        def subtract(c):
+            nc.vector.tensor_tensor(out=diff[c][:], in0=p_bank[c][:], in1=q_sb[c][:], op=ALU.subtract)
+
+        def bend(c):
+            nc.scalar.activation(out=bent[c][:], in_=diff[c][:], func=ACT.Tanh)
+
+        def add(c):
+            nc.vector.tensor_tensor(out=y[c][:].rearrange("p t j -> p (t j)"), in0=p_bank[c][:], in1=bent[c][:], op=ALU.add)
+            nc.sync.dma_start(out=y_rows[:, :, c * CHUNK : (c + 1) * CHUNK], in_=y[c][:])
+
+        def round_y(c):
+            place = last_woven[:] if c == last else early_woven[:, c * CHUNK : (c + 1) * CHUNK, :]
+            dst = place.rearrange("p (b i) t -> p b t i", i=4)
+            src = y[c][:].rearrange("p t (b i) -> p b t i", i=4)
+            if c == last:
+                nc.vector.tensor_copy(out=dst, in_=src)
+            elif c == last - 1:
+                nc.scalar.copy(out=dst, in_=src)
+            else:
+                nc.gpsimd.tensor_scalar(out=dst, in0=src, scalar1=1.0, scalar2=0.0, op0=ALU.mult, op1=ALU.add)
+
+        def quantise_y(woven_y, cols):
+            codes = keep.tile([P, cols.stop - cols.start], U32, name="y_codes%d" % cols.start, align_bytes=64)
+            nc.vector.quantize_mx(out=codes[:].bitcast(FP8X4), scales=y_scale[:, cols], in_=woven_y[:].rearrange("p j t -> p (j t)"))
+            nc.sync.dma_start(out=words[:, cols], in_=codes[:].bitcast(I32))
+
+        fetch_q(0)
+        subtract(0)
+        for c in range(CHUNKS):
+            if c < last:
+                fetch_q(c + 1)
+            bend(c)
+            if c < last:
+                subtract(c + 1)
+            if c == last:
+                round_y(c - 1)
+            add(c)
+            if c != last - 1:
+                round_y(c)
+        quantise_y(early_woven, slice(0, last * CHUNK))
+        quantise_y(last_woven, slice(last * CHUNK, J))
+        for quad in range(QUADS):
+            queue = nc.sync if quad % 2 == 0 else nc.scalar
+            queue.dma_start(
+                out=out_2[0, 4 * quad : 4 * quad + 4, :].bitcast(I32),
+                in_=y_scale[32 * quad : 32 * quad + 4, :].bitcast(I32),
+            )

@@ -24,7 +24,7 @@ CHUNKS = J // CHUNK
 LIST_COLS = CHUNK // 16
 QUADS = 4
 WB_ROW = 4
-ROWS_BEFORE_WEIGHTS = 6
+ROWS_BEFORE_WEIGHTS = 7
 
 
 def tile_list_expert_contrast_pl_kernel(tc, xq, wa_words, wa_scales, wb_words, wb_scales, offs, out_0, out_1, out_2):
@@ -43,10 +43,22 @@ def tile_list_expert_contrast_pl_kernel(tc, xq, wa_words, wa_scales, wb_words, w
         def load_x(i):
             nc.sync.dma_start(out=x_rows[i][:], in_=xq_rows[i // PACK, i % PACK])
 
+        def load_scales(scales, row, quad):
+            first = 32 * quad + row
+            nc.sync.dma_start(
+                out=scale_raw[first : first + 4, :].bitcast(I32).rearrange("r (g n) -> r g n", g=PASSES),
+                in_=scales[:, 4 * quad : 4 * quad + 4, :].rearrange("g r n -> r g n").bitcast(I32),
+            )
+
+        nc.vector.memset(scale_raw[:].bitcast(I32), 0)
+        scale_loads = [(s, row, quad) for s, row in ((wb_scales, WB_ROW), (wa_scales, 0)) for quad in range(QUADS)]
         load_x(0)
         nc.sync.dma_start(offsets[:], offs)
         for i in range(1, ROWS_BEFORE_WEIGHTS):
             load_x(i)
+            load_scales(*scale_loads[i - 1])
+        for item in scale_loads[ROWS_BEFORE_WEIGHTS - 1 :]:
+            load_scales(*item)
         nc.sync.dma_start(
             out=wb_raw[:].bitcast(I32).rearrange("p (g n) -> p g n", g=PASSES),
             in_=wb_words.rearrange("g p n t -> p g (n t)").bitcast(I32),
@@ -57,15 +69,6 @@ def tile_list_expert_contrast_pl_kernel(tc, xq, wa_words, wa_scales, wb_words, w
         )
         for i in range(ROWS_BEFORE_WEIGHTS, PASSES * PACK):
             load_x(i)
-
-        nc.gpsimd.memset(scale_raw[:].bitcast(I32), 0)
-        for scales, row in ((wa_scales, 0), (wb_scales, WB_ROW)):
-            for quad in range(QUADS):
-                first = 32 * quad + row
-                nc.gpsimd.dma_start(
-                    out=scale_raw[first : first + 4, :].bitcast(I32).rearrange("r (g n) -> r g n", g=PASSES),
-                    in_=scales[:, 4 * quad : 4 * quad + 4, :].rearrange("g r n -> r g n").bitcast(I32),
-                )
 
         w_scale = keep.tile([P, PASSES * N], U8, name="w_scale", align_bytes=64)
 
@@ -88,18 +91,18 @@ def tile_list_expert_contrast_pl_kernel(tc, xq, wa_words, wa_scales, wb_words, w
 
         def deal_weights(g):
             nc.vector.tensor_copy(
-                out=wb_dealt[g][:].rearrange("p (t m) -> p m t", t=PACK),
-                in_=wb_raw[:, g * N : (g + 1) * N].rearrange("p (m t) -> p m t", t=PACK),
+                out=wb_dealt[g][:].rearrange("p (t b i) -> p b t i", t=PACK, i=4),
+                in_=wb_raw[:, g * N : (g + 1) * N].rearrange("p (b i t) -> p b t i", t=PACK, i=4),
             )
             nc.scalar.copy(
-                out=wa_dealt[g][:].bitcast(U16).rearrange("p (t m) -> p m t", t=PACK),
-                in_=wa_raw[:, g * 2 * N : (g + 1) * 2 * N].bitcast(U16).rearrange("p (m t) -> p m t", t=PACK),
+                out=wa_dealt[g][:].bitcast(U16).rearrange("p (t b i) -> p b t i", t=PACK, i=8),
+                in_=wa_raw[:, g * 2 * N : (g + 1) * 2 * N].bitcast(U16).rearrange("p (b i t) -> p b t i", t=PACK, i=8),
             )
 
         p_bank = [psum.tile([P, PACK * CHUNK], F32, name="p_bank%d" % c) for c in range(CHUNKS)]
         q_bank = [psum.tile([P, PACK * CHUNK], F32, name="q_bank%d" % c) for c in range(CHUNKS)]
 
-        def multiply(g, c):
+        def multiply_q(g, c):
             for t in range(PACK):
                 cols = slice(g * N + t * P, g * N + (t + 1) * P)
                 nc.tensor.matmul_mx(
@@ -111,6 +114,8 @@ def tile_list_expert_contrast_pl_kernel(tc, xq, wa_words, wa_scales, wb_words, w
                     start=(g == 0 and t == 0),
                     stop=(g == PASSES - 1 and t == PACK - 1),
                 )
+
+        def multiply_p(g, c):
             for t in range(PACK):
                 cols = slice(g * N + t * P, g * N + (t + 1) * P)
                 nc.tensor.matmul_mx(
@@ -132,13 +137,15 @@ def tile_list_expert_contrast_pl_kernel(tc, xq, wa_words, wa_scales, wb_words, w
                 window = x_rows[g * PACK + t]
                 if g * PACK + t == ROWS_BEFORE_WEIGHTS:
                     nc.vector.tensor_copy(
-                        out=w_scale[:].rearrange("p (g t m) -> p g m t", g=PASSES, t=PACK),
-                        in_=scale_raw[:].rearrange("p (g m t) -> p g m t", g=PASSES, t=PACK),
+                        out=w_scale[:].rearrange("p (g t b i) -> p g b t i", g=PASSES, t=PACK, i=16),
+                        in_=scale_raw[:].rearrange("p (g b i t) -> p g b t i", g=PASSES, t=PACK, i=16),
                     )
                     for h in range(PASSES):
                         deal_weights(h)
                     for c in range(CHUNKS):
-                        multiply(0, c)
+                        multiply_q(0, c)
+                    for c in range(CHUNKS):
+                        multiply_p(0, c)
                 nc.vector.tensor_copy(out=inner_woven[:, :, t], in_=window[:].indirect(listed(1, 2)))
                 for c in outer:
                     nc.scalar.activation(out=picked[c][:, t, :], in_=window[:].indirect(listed(c, 1)), func=ACT.Copy)
@@ -150,7 +157,8 @@ def tile_list_expert_contrast_pl_kernel(tc, xq, wa_words, wa_scales, wb_words, w
             quantise_x(g, outer[1], 1, woven[outer[1]])
 
         for c in range(CHUNKS):
-            multiply(PASSES - 1, c)
+            multiply_q(PASSES - 1, c)
+            multiply_p(PASSES - 1, c)
 
         y_rows = out_0.rearrange("(p t) j -> p t j", t=PACK)
         words = out_1[0].rearrange("p j t -> p (j t)").bitcast(I32)
@@ -160,8 +168,8 @@ def tile_list_expert_contrast_pl_kernel(tc, xq, wa_words, wa_scales, wb_words, w
         bent = [keep.tile([P, PACK * CHUNK], F32, name="bent%d" % c) for c in range(CHUNKS)]
         y = [keep.tile([P, PACK, CHUNK], F32, name="y%d" % c) for c in range(CHUNKS)]
         last = CHUNKS - 1
-        early_woven = keep.tile([P, last * CHUNK, PACK], BF16, name="early_woven", align_bytes=64)
-        last_woven = keep.tile([P, CHUNK, PACK], BF16, name="last_woven", align_bytes=64)
+        HALF = CHUNKS // 2
+        y_woven = [keep.tile([P, HALF * CHUNK, PACK], BF16, name="y_woven%d" % h, align_bytes=64) for h in range(2)]
 
         def fetch_q(c):
             nc.scalar.copy(out=q_sb[c][:], in_=q_bank[c][:])
@@ -177,15 +185,13 @@ def tile_list_expert_contrast_pl_kernel(tc, xq, wa_words, wa_scales, wb_words, w
             nc.sync.dma_start(out=y_rows[:, :, c * CHUNK : (c + 1) * CHUNK], in_=y[c][:])
 
         def round_y(c):
-            place = last_woven[:] if c == last else early_woven[:, c * CHUNK : (c + 1) * CHUNK, :]
+            place = y_woven[c // HALF][:, (c % HALF) * CHUNK : (c % HALF + 1) * CHUNK, :]
             dst = place.rearrange("p (b i) t -> p b t i", i=4)
             src = y[c][:].rearrange("p t (b i) -> p b t i", i=4)
-            if c == last:
+            if c >= HALF:
                 nc.vector.tensor_copy(out=dst, in_=src)
-            elif c == last - 1:
-                nc.scalar.copy(out=dst, in_=src)
             else:
-                nc.gpsimd.tensor_scalar(out=dst, in0=src, scalar1=1.0, scalar2=0.0, op0=ALU.mult, op1=ALU.add)
+                nc.scalar.copy(out=dst, in_=src)
 
         def quantise_y(woven_y, cols):
             codes = keep.tile([P, cols.stop - cols.start], U32, name="y_codes%d" % cols.start, align_bytes=64)
@@ -200,13 +206,11 @@ def tile_list_expert_contrast_pl_kernel(tc, xq, wa_words, wa_scales, wb_words, w
             bend(c)
             if c < last:
                 subtract(c + 1)
-            if c == last:
-                round_y(c - 1)
             add(c)
-            if c != last - 1:
-                round_y(c)
-        quantise_y(early_woven, slice(0, last * CHUNK))
-        quantise_y(last_woven, slice(last * CHUNK, J))
+        for c in range(CHUNKS):
+            round_y(c)
+        for h in range(2):
+            quantise_y(y_woven[h], slice(h * HALF * CHUNK, (h + 1) * HALF * CHUNK))
         for quad in range(QUADS):
             queue = nc.sync if quad % 2 == 0 else nc.scalar
             queue.dma_start(

@@ -24,7 +24,8 @@ CHUNKS = J // CHUNK
 LIST_COLS = CHUNK // 16
 QUADS = 4
 WB_ROW = 4
-ROWS_BEFORE_WEIGHTS = 7
+ROWS_BEFORE_WB = 6
+ROWS_BEFORE_WA = 7
 
 
 def tile_list_expert_contrast_pl_kernel(tc, xq, wa_words, wa_scales, wb_words, wb_scales, offs, out_0, out_1, out_2):
@@ -54,21 +55,22 @@ def tile_list_expert_contrast_pl_kernel(tc, xq, wa_words, wa_scales, wb_words, w
         scale_loads = [(s, row, quad) for s, row in ((wb_scales, WB_ROW), (wa_scales, 0)) for quad in range(QUADS)]
         load_x(0)
         nc.sync.dma_start(offsets[:], offs)
-        for i in range(1, ROWS_BEFORE_WEIGHTS):
+        for i in range(1, PASSES * PACK):
+            if i == ROWS_BEFORE_WB:
+                nc.sync.dma_start(
+                    out=wb_raw[:].bitcast(I32).rearrange("p (g n) -> p g n", g=PASSES),
+                    in_=wb_words.rearrange("g p n t -> p g (n t)").bitcast(I32),
+                )
+                for item in scale_loads[i - 1 :]:
+                    load_scales(*item)
+            if i == ROWS_BEFORE_WA:
+                nc.sync.dma_start(
+                    out=wa_raw[:].bitcast(I32).rearrange("p (g n) -> p g n", g=PASSES),
+                    in_=wa_words.rearrange("g p n -> p g n").bitcast(I32),
+                )
             load_x(i)
-            load_scales(*scale_loads[i - 1])
-        for item in scale_loads[ROWS_BEFORE_WEIGHTS - 1 :]:
-            load_scales(*item)
-        nc.sync.dma_start(
-            out=wb_raw[:].bitcast(I32).rearrange("p (g n) -> p g n", g=PASSES),
-            in_=wb_words.rearrange("g p n t -> p g (n t)").bitcast(I32),
-        )
-        nc.sync.dma_start(
-            out=wa_raw[:].bitcast(I32).rearrange("p (g n) -> p g n", g=PASSES),
-            in_=wa_words.rearrange("g p n -> p g n").bitcast(I32),
-        )
-        for i in range(ROWS_BEFORE_WEIGHTS, PASSES * PACK):
-            load_x(i)
+            if i < ROWS_BEFORE_WB:
+                load_scales(*scale_loads[i - 1])
 
         w_scale = keep.tile([P, PASSES * N], U8, name="w_scale", align_bytes=64)
 
@@ -78,7 +80,7 @@ def tile_list_expert_contrast_pl_kernel(tc, xq, wa_words, wa_scales, wb_words, w
         def quantise_x(g, first, count, woven):
             codes = keep.tile([P, count * CHUNK], U32, name="x_codes%d_%d" % (g, first), align_bytes=64)
             scale = keep.tile([P, count * CHUNK], U8, name="x_scale%d_%d" % (g, first), align_bytes=64)
-            nc.vector.quantize_mx(out=codes[:].bitcast(FP8X4), scales=scale[:], in_=woven[:].rearrange("p j t -> p (j t)"))
+            nc.vector.quantize_mx(out=codes[:].bitcast(FP8X4), scales=scale[:], in_=woven.rearrange("p j t -> p (j t)"))
             for c in range(count):
                 x_codes[g, first + c] = codes[:, c * CHUNK : (c + 1) * CHUNK]
                 x_scale[g, first + c] = scale[:, c * CHUNK : (c + 1) * CHUNK]
@@ -89,11 +91,13 @@ def tile_list_expert_contrast_pl_kernel(tc, xq, wa_words, wa_scales, wb_words, w
         wa_dealt = [keep.tile([P, 2 * N], U8, name="wa_dealt%d" % g, align_bytes=64) for g in range(PASSES)]
         wb_dealt = [keep.tile([P, N], U32, name="wb_dealt%d" % g, align_bytes=64) for g in range(PASSES)]
 
-        def deal_weights(g):
+        def deal_wb(g):
             nc.vector.tensor_copy(
                 out=wb_dealt[g][:].rearrange("p (t b i) -> p b t i", t=PACK, i=4),
                 in_=wb_raw[:, g * N : (g + 1) * N].rearrange("p (b i t) -> p b t i", t=PACK, i=4),
             )
+
+        def deal_wa(g):
             nc.scalar.copy(
                 out=wa_dealt[g][:].bitcast(U16).rearrange("p (t b i) -> p b t i", t=PACK, i=8),
                 in_=wa_raw[:, g * 2 * N : (g + 1) * 2 * N].bitcast(U16).rearrange("p (b i t) -> p b t i", t=PACK, i=8),
@@ -128,48 +132,50 @@ def tile_list_expert_contrast_pl_kernel(tc, xq, wa_words, wa_scales, wb_words, w
                     stop=(g == PASSES - 1 and t == PACK - 1),
                 )
 
-        outer = (0, CHUNKS - 1)
+        HALF = CHUNKS // 2
         for g in range(PASSES):
-            inner_woven = keep.tile([P, 2 * CHUNK, PACK], BF16, name="inner_woven%d" % g, align_bytes=64)
-            picked = {c: keep.tile([P, PACK, CHUNK], BF16, name="picked%d_%d" % (g, c)) for c in outer}
-            woven = {c: keep.tile([P, CHUNK, PACK], BF16, name="woven%d_%d" % (g, c), align_bytes=64) for c in outer}
+            front_woven = keep.tile([P, HALF * CHUNK, PACK], BF16, name="front_woven%d" % g, align_bytes=64)
+            back_picked = keep.tile([P, PACK, HALF * CHUNK], BF16, name="back_picked%d" % g)
+            back_woven = keep.tile([P, HALF * CHUNK, PACK], BF16, name="back_woven%d" % g, align_bytes=64)
             for t in range(PACK):
                 window = x_rows[g * PACK + t]
-                if g * PACK + t == ROWS_BEFORE_WEIGHTS:
+                if g * PACK + t == ROWS_BEFORE_WB:
                     nc.vector.tensor_copy(
                         out=w_scale[:].rearrange("p (g t b i) -> p g b t i", g=PASSES, t=PACK, i=16),
                         in_=scale_raw[:].rearrange("p (g b i t) -> p g b t i", g=PASSES, t=PACK, i=16),
                     )
                     for h in range(PASSES):
-                        deal_weights(h)
+                        deal_wb(h)
                     for c in range(CHUNKS):
                         multiply_q(0, c)
+                if g * PACK + t == ROWS_BEFORE_WA:
+                    for h in range(PASSES):
+                        deal_wa(h)
                     for c in range(CHUNKS):
                         multiply_p(0, c)
-                nc.vector.tensor_copy(out=inner_woven[:, :, t], in_=window[:].indirect(listed(1, 2)))
-                for c in outer:
-                    nc.scalar.activation(out=picked[c][:, t, :], in_=window[:].indirect(listed(c, 1)), func=ACT.Copy)
-                    if t >= PACK - 2:
-                        rows = slice(0, PACK - 1) if t == PACK - 2 else slice(t, PACK)
-                        nc.scalar.copy(out=woven[c][:, :, rows], in_=picked[c][:, rows, :].rearrange("p t j -> p j t"))
-            quantise_x(g, outer[0], 1, woven[outer[0]])
-            quantise_x(g, 1, 2, inner_woven)
-            quantise_x(g, outer[1], 1, woven[outer[1]])
+                nc.vector.tensor_copy(out=front_woven[:, :, t], in_=window[:].indirect(listed(0, HALF)))
+                nc.scalar.activation(out=back_picked[:, t, :], in_=window[:].indirect(listed(HALF, HALF)), func=ACT.Copy)
+                if t >= PACK - 2:
+                    rows = slice(0, PACK - 1) if t == PACK - 2 else slice(t, PACK)
+                    nc.scalar.copy(out=back_woven[:, :, rows], in_=back_picked[:, rows, :].rearrange("p t j -> p j t"))
+            for c in range(HALF):
+                quantise_x(g, c, 1, front_woven[:, c * CHUNK : (c + 1) * CHUNK, :])
+            quantise_x(g, HALF, HALF, back_woven[:])
 
+        multiply_q(PASSES - 1, 0)
         for c in range(CHUNKS):
-            multiply_q(PASSES - 1, c)
+            if c + 1 < CHUNKS:
+                multiply_q(PASSES - 1, c + 1)
             multiply_p(PASSES - 1, c)
 
         y_rows = out_0.rearrange("(p t) j -> p t j", t=PACK)
         words = out_1[0].rearrange("p j t -> p (j t)").bitcast(I32)
         y_scale = keep.tile([P, J], U8, name="y_scale", align_bytes=64)
         q_sb = [keep.tile([P, PACK * CHUNK], F32, name="q_sb%d" % c) for c in range(CHUNKS)]
-        diff = [keep.tile([P, PACK * CHUNK], F32, name="diff%d" % c) for c in range(CHUNKS)]
-        bent = [keep.tile([P, PACK * CHUNK], F32, name="bent%d" % c) for c in range(CHUNKS)]
+        diff = [keep.tile([P, PACK * CHUNK], F32, name="diff%d" % c, tag="diff%d" % c, align_bytes=64) for c in range(CHUNKS)]
+        bent = [keep.tile([P, PACK * CHUNK], F32, name="bent%d" % c, tag="bent%d" % c, align_bytes=64) for c in range(CHUNKS)]
         y = [keep.tile([P, PACK, CHUNK], F32, name="y%d" % c) for c in range(CHUNKS)]
         last = CHUNKS - 1
-        HALF = CHUNKS // 2
-        y_woven = [keep.tile([P, HALF * CHUNK, PACK], BF16, name="y_woven%d" % h, align_bytes=64) for h in range(2)]
 
         def fetch_q(c):
             nc.scalar.copy(out=q_sb[c][:], in_=q_bank[c][:])
@@ -184,35 +190,42 @@ def tile_list_expert_contrast_pl_kernel(tc, xq, wa_words, wa_scales, wb_words, w
             nc.vector.tensor_tensor(out=y[c][:].rearrange("p t j -> p (t j)"), in0=p_bank[c][:], in1=bent[c][:], op=ALU.add)
             nc.sync.dma_start(out=y_rows[:, :, c * CHUNK : (c + 1) * CHUNK], in_=y[c][:])
 
-        def round_y(c):
-            place = y_woven[c // HALF][:, (c % HALF) * CHUNK : (c % HALF + 1) * CHUNK, :]
-            dst = place.rearrange("p (b i) t -> p b t i", i=4)
-            src = y[c][:].rearrange("p t (b i) -> p b t i", i=4)
-            if c >= HALF:
-                nc.vector.tensor_copy(out=dst, in_=src)
-            else:
-                nc.scalar.copy(out=dst, in_=src)
+        def quantise_y(woven_y, codes, first, count):
+            cols = slice(first * CHUNK, (first + count) * CHUNK)
+            nc.vector.quantize_mx(out=codes.bitcast(FP8X4), scales=y_scale[:, cols], in_=woven_y[:].rearrange("p j t -> p (j t)"))
 
-        def quantise_y(woven_y, cols):
-            codes = keep.tile([P, cols.stop - cols.start], U32, name="y_codes%d" % cols.start, align_bytes=64)
-            nc.vector.quantize_mx(out=codes[:].bitcast(FP8X4), scales=y_scale[:, cols], in_=woven_y[:].rearrange("p j t -> p (j t)"))
-            nc.sync.dma_start(out=words[:, cols], in_=codes[:].bitcast(I32))
-
-        fetch_q(0)
-        subtract(0)
-        for c in range(CHUNKS):
-            if c < last:
-                fetch_q(c + 1)
-            bend(c)
-            if c < last:
-                subtract(c + 1)
-            add(c)
-        for c in range(CHUNKS):
-            round_y(c)
-        for h in range(2):
-            quantise_y(y_woven[h], slice(h * HALF * CHUNK, (h + 1) * HALF * CHUNK))
+        AHEAD = 2
+        for step in range(CHUNKS + AHEAD):
+            if step < CHUNKS:
+                fetch_q(step)
+                subtract(step)
+            if step >= AHEAD:
+                bend(step - AHEAD)
+                add(step - AHEAD)
+        front_y = keep.tile([P, HALF * CHUNK, PACK], BF16, name="front_y", tag="front_y", align_bytes=64)
+        for c in range(HALF):
+            nc.gpsimd.tensor_scalar(
+                out=front_y[:, c * CHUNK : (c + 1) * CHUNK, :],
+                in0=y[c][:].rearrange("p t j -> p j t"),
+                scalar1=1.0,
+                scalar2=0.0,
+                op0=ALU.mult,
+                op1=ALU.add,
+            )
+        front_codes = keep.tile([P, HALF * CHUNK], U32, name="front_codes", tag="bent%d" % last, align_bytes=64)
+        quantise_y(front_y, front_codes[:], 0, HALF)
+        nc.sync.dma_start(out=words[:, : HALF * CHUNK], in_=front_codes[:].bitcast(I32))
+        back_codes = keep.tile([P, HALF * CHUNK], U32, name="back_codes", tag="front_y", align_bytes=64)
+        for c in range(HALF, CHUNKS):
+            back_y = keep.tile([P, CHUNK, PACK], BF16, name="back_y%d" % c, tag=("diff%d" % last if c == HALF else "back_y"), align_bytes=64)
+            nc.scalar.copy(
+                out=back_y[:].rearrange("p (b i) t -> p b t i", i=4),
+                in_=y[c][:].rearrange("p t (b i) -> p b t i", i=4),
+            )
+            quantise_y(back_y, back_codes[:, (c - HALF) * CHUNK : (c - HALF + 1) * CHUNK], c, 1)
+        nc.sync.dma_start(out=words[:, HALF * CHUNK :], in_=back_codes[:].bitcast(I32))
         for quad in range(QUADS):
-            queue = nc.sync if quad % 2 == 0 else nc.scalar
+            queue = nc.scalar if quad < 2 else nc.sync
             queue.dma_start(
                 out=out_2[0, 4 * quad : 4 * quad + 4, :].bitcast(I32),
                 in_=y_scale[32 * quad : 32 * quad + 4, :].bitcast(I32),

@@ -24,8 +24,6 @@ CHUNKS = J // CHUNK
 LIST_COLS = CHUNK // 16
 QUADS = 4
 WB_ROW = 4
-ROWS_BEFORE_WB = 6
-ROWS_BEFORE_WA = 7
 
 
 def tile_list_expert_contrast_pl_kernel(tc, xq, wa_words, wa_scales, wb_words, wb_scales, offs, out_0, out_1, out_2):
@@ -35,42 +33,46 @@ def tile_list_expert_contrast_pl_kernel(tc, xq, wa_words, wa_scales, wb_words, w
         psum = ctx.enter_context(tc.psum_pool(name="psum", bufs=1))
 
         offsets = keep.tile([P, J // 16], U16, name="offsets")
-        x_rows = [keep.tile([P, T], F32, name="x_rows%d" % i) for i in range(PASSES * PACK)]
-        wa_raw = keep.tile([P, PASSES * 2 * N], U8, name="wa_raw", align_bytes=64)
-        wb_raw = keep.tile([P, PASSES * N], U32, name="wb_raw", align_bytes=64)
+        wa_raw = [keep.tile([P, 2 * N], U8, name="wa_raw%d" % g, align_bytes=64) for g in range(PASSES)]
+        wb_raw = [keep.tile([P, N], U32, name="wb_raw%d" % g, align_bytes=64) for g in range(PASSES)]
         scale_raw = keep.tile([P, PASSES * N], U8, name="scale_raw", align_bytes=64)
-        xq_rows = xq.rearrange("(g p t) c -> g t p c", p=P, t=PACK)
+        xq_rows = xq.rearrange("(g p t) c -> g p t c", p=P, t=PACK)
+        x_rows = {}
 
-        def load_x(i):
-            nc.sync.dma_start(out=x_rows[i][:], in_=xq_rows[i // PACK, i % PACK])
+        def load_x(g, first, count):
+            rows = keep.tile([P, count * T], F32, name="x_rows%d_%d" % (g, first))
+            nc.sync.dma_start(out=rows[:].rearrange("p (t c) -> p t c", t=count), in_=xq_rows[g, :, first : first + count, :])
+            for t in range(count):
+                x_rows[g, first + t] = rows[:, t * T : (t + 1) * T]
 
-        def load_scales(scales, row, quad):
-            first = 32 * quad + row
-            nc.sync.dma_start(
-                out=scale_raw[first : first + 4, :].bitcast(I32).rearrange("r (g n) -> r g n", g=PASSES),
-                in_=scales[:, 4 * quad : 4 * quad + 4, :].rearrange("g r n -> r g n").bitcast(I32),
-            )
+        def load_wb(g):
+            nc.sync.dma_start(out=wb_raw[g][:].bitcast(I32), in_=wb_words[g].rearrange("p n t -> p (n t)").bitcast(I32))
 
-        nc.vector.memset(scale_raw[:].bitcast(I32), 0)
-        scale_loads = [(s, row, quad) for s, row in ((wb_scales, WB_ROW), (wa_scales, 0)) for quad in range(QUADS)]
-        load_x(0)
+        def load_wa(g):
+            nc.sync.dma_start(out=wa_raw[g][:].bitcast(I32), in_=wa_words[g].bitcast(I32))
+
+        load_x(0, 0, 2)
         nc.sync.dma_start(offsets[:], offs)
-        for i in range(1, PASSES * PACK):
-            if i == ROWS_BEFORE_WB:
-                nc.sync.dma_start(
-                    out=wb_raw[:].bitcast(I32).rearrange("p (g n) -> p g n", g=PASSES),
-                    in_=wb_words.rearrange("g p n t -> p g (n t)").bitcast(I32),
+        load_x(0, 2, 2)
+        load_x(1, 0, 2)
+        load_wb(1)
+        load_wa(1)
+        split_rows = keep.tile([P, T], F32, name="split_rows")
+        x_rows[1, 2] = split_rows[:]
+        nc.sync.dma_start(out=split_rows[:, : T // 2], in_=xq_rows[1, :, 2, : T // 2])
+        load_wb(0)
+        nc.sync.dma_start(out=split_rows[:, T // 2 :], in_=xq_rows[1, :, 2, T // 2 :])
+        load_wa(0)
+        load_x(1, 3, 1)
+
+        nc.gpsimd.memset(scale_raw[:].bitcast(I32), 0)
+        for scales, row in ((wb_scales, WB_ROW), (wa_scales, 0)):
+            for quad in range(QUADS):
+                first = 32 * quad + row
+                nc.gpsimd.dma_start(
+                    out=scale_raw[first : first + 4, :].bitcast(I32).rearrange("r (g n) -> r g n", g=PASSES),
+                    in_=scales[:, 4 * quad : 4 * quad + 4, :].rearrange("g r n -> r g n").bitcast(I32),
                 )
-                for item in scale_loads[i - 1 :]:
-                    load_scales(*item)
-            if i == ROWS_BEFORE_WA:
-                nc.sync.dma_start(
-                    out=wa_raw[:].bitcast(I32).rearrange("p (g n) -> p g n", g=PASSES),
-                    in_=wa_words.rearrange("g p n -> p g n").bitcast(I32),
-                )
-            load_x(i)
-            if i < ROWS_BEFORE_WB:
-                load_scales(*scale_loads[i - 1])
 
         w_scale = keep.tile([P, PASSES * N], U8, name="w_scale", align_bytes=64)
 
@@ -94,13 +96,13 @@ def tile_list_expert_contrast_pl_kernel(tc, xq, wa_words, wa_scales, wb_words, w
         def deal_wb(g):
             nc.vector.tensor_copy(
                 out=wb_dealt[g][:].rearrange("p (t b i) -> p b t i", t=PACK, i=4),
-                in_=wb_raw[:, g * N : (g + 1) * N].rearrange("p (b i t) -> p b t i", t=PACK, i=4),
+                in_=wb_raw[g][:].rearrange("p (b i t) -> p b t i", t=PACK, i=4),
             )
 
         def deal_wa(g):
             nc.scalar.copy(
                 out=wa_dealt[g][:].bitcast(U16).rearrange("p (t b i) -> p b t i", t=PACK, i=8),
-                in_=wa_raw[:, g * 2 * N : (g + 1) * 2 * N].bitcast(U16).rearrange("p (b i t) -> p b t i", t=PACK, i=8),
+                in_=wa_raw[g][:].bitcast(U16).rearrange("p (b i t) -> p b t i", t=PACK, i=8),
             )
 
         p_bank = [psum.tile([P, PACK * CHUNK], F32, name="p_bank%d" % c) for c in range(CHUNKS)]
@@ -133,34 +135,45 @@ def tile_list_expert_contrast_pl_kernel(tc, xq, wa_words, wa_scales, wb_words, w
                 )
 
         HALF = CHUNKS // 2
-        for g in range(PASSES):
-            front_woven = keep.tile([P, HALF * CHUNK, PACK], BF16, name="front_woven%d" % g, align_bytes=64)
-            back_picked = keep.tile([P, PACK, HALF * CHUNK], BF16, name="back_picked%d" % g)
-            back_woven = keep.tile([P, HALF * CHUNK, PACK], BF16, name="back_woven%d" % g, align_bytes=64)
-            for t in range(PACK):
-                window = x_rows[g * PACK + t]
-                if g * PACK + t == ROWS_BEFORE_WB:
-                    nc.vector.tensor_copy(
-                        out=w_scale[:].rearrange("p (g t b i) -> p g b t i", g=PASSES, t=PACK, i=16),
-                        in_=scale_raw[:].rearrange("p (g b i t) -> p g b t i", g=PASSES, t=PACK, i=16),
-                    )
-                    for h in range(PASSES):
-                        deal_wb(h)
-                    for c in range(CHUNKS):
-                        multiply_q(0, c)
-                if g * PACK + t == ROWS_BEFORE_WA:
-                    for h in range(PASSES):
-                        deal_wa(h)
-                    for c in range(CHUNKS):
-                        multiply_p(0, c)
-                nc.vector.tensor_copy(out=front_woven[:, :, t], in_=window[:].indirect(listed(0, HALF)))
-                nc.scalar.activation(out=back_picked[:, t, :], in_=window[:].indirect(listed(HALF, HALF)), func=ACT.Copy)
-                if t >= PACK - 2:
-                    rows = slice(0, PACK - 1) if t == PACK - 2 else slice(t, PACK)
-                    nc.scalar.copy(out=back_woven[:, :, rows], in_=back_picked[:, rows, :].rearrange("p t j -> p j t"))
+        front_woven = [keep.tile([P, HALF * CHUNK, PACK], BF16, name="front_woven%d" % g, align_bytes=64) for g in range(PASSES)]
+        back_picked = [keep.tile([P, PACK, HALF * CHUNK], F32, name="back_picked%d" % g) for g in range(PASSES)]
+        back_woven = [keep.tile([P, HALF * CHUNK, PACK], BF16, name="back_woven%d" % g, align_bytes=64) for g in range(PASSES)]
+
+        def gather(g, t):
+            nc.vector.tensor_copy(out=front_woven[g][:, :, t], in_=x_rows[g, t].indirect(listed(0, HALF)))
+            nc.scalar.activation(out=back_picked[g][:, t, :], in_=x_rows[g, t].indirect(listed(HALF, HALF)), func=ACT.Copy)
+
+        def weave_back(g, rows):
+            nc.scalar.copy(out=back_woven[g][:, :, rows], in_=back_picked[g][:, rows, :].rearrange("p t j -> p j t"))
+
+        def quantise_pass(g):
             for c in range(HALF):
-                quantise_x(g, c, 1, front_woven[:, c * CHUNK : (c + 1) * CHUNK, :])
-            quantise_x(g, HALF, HALF, back_woven[:])
+                quantise_x(g, c, 1, front_woven[g][:, c * CHUNK : (c + 1) * CHUNK, :])
+            quantise_x(g, HALF, HALF, back_woven[g][:])
+
+        for t in range(PACK):
+            gather(0, t)
+        weave_back(0, slice(0, PACK))
+        nc.vector.tensor_copy(
+            out=w_scale[:].rearrange("p (g t b i) -> p g b t i", g=PASSES, t=PACK, i=16),
+            in_=scale_raw[:].rearrange("p (g b i t) -> p g b t i", g=PASSES, t=PACK, i=16),
+        )
+        quantise_pass(0)
+        gather(1, 0)
+        gather(1, 1)
+        deal_wb(1)
+        deal_wa(1)
+        deal_wb(0)
+        gather(1, 2)
+        deal_wa(0)
+        weave_back(1, slice(0, PACK - 1))
+        for c in range(CHUNKS):
+            multiply_q(0, c)
+        for c in range(CHUNKS):
+            multiply_p(0, c)
+        gather(1, PACK - 1)
+        weave_back(1, slice(PACK - 1, PACK))
+        quantise_pass(1)
 
         multiply_q(PASSES - 1, 0)
         for c in range(CHUNKS):

@@ -34,7 +34,7 @@ def tile_list_expert_contrast_pl_kernel(tc, xq, wa_words, wa_scales, wb_words, w
 
         offsets = keep.tile([P, J // 16], U16, name="offsets")
         wa_raw = [keep.tile([P, 2 * N], U8, name="wa_raw%d" % g, align_bytes=64) for g in range(PASSES)]
-        wb_raw = [keep.tile([P, N], U32, name="wb_raw%d" % g, align_bytes=64) for g in range(PASSES)]
+        wb_raw = [keep.tile([P, N], U32, name="wb_raw%d" % g, tag="wb_raw%d" % g, align_bytes=64) for g in range(PASSES)]
         scale_raw = keep.tile([P, PASSES * N], U8, name="scale_raw", align_bytes=64)
         xq_rows = xq.rearrange("(g p t) c -> g p t c", p=P, t=PACK)
         x_rows = {}
@@ -74,7 +74,6 @@ def tile_list_expert_contrast_pl_kernel(tc, xq, wa_words, wa_scales, wb_words, w
                     in_=scales[:, 4 * quad : 4 * quad + 4, :].rearrange("g r n -> r g n").bitcast(I32),
                 )
 
-        w_scale = keep.tile([P, PASSES * N], U8, name="w_scale", align_bytes=64)
 
         x_codes = {}
         x_scale = {}
@@ -154,14 +153,15 @@ def tile_list_expert_contrast_pl_kernel(tc, xq, wa_words, wa_scales, wb_words, w
         for t in range(PACK):
             gather(0, t)
         weave_back(0, slice(0, PACK))
-        nc.vector.tensor_copy(
-            out=w_scale[:].rearrange("p (g t b i) -> p g b t i", g=PASSES, t=PACK, i=16),
-            in_=scale_raw[:].rearrange("p (g b i t) -> p g b t i", g=PASSES, t=PACK, i=16),
-        )
         quantise_pass(0)
         gather(1, 0)
         gather(1, 1)
         deal_wb(1)
+        w_scale = keep.tile([P, PASSES * N], U8, name="w_scale", tag="wb_raw1", align_bytes=64)
+        nc.vector.tensor_copy(
+            out=w_scale[:].rearrange("p (g t b i) -> p g b t i", g=PASSES, t=PACK, i=16),
+            in_=scale_raw[:].rearrange("p (g b i t) -> p g b t i", g=PASSES, t=PACK, i=16),
+        )
         deal_wa(1)
         deal_wb(0)
         gather(1, 2)

from contextlib import ExitStack

import concourse.mybir as mybir

K, T, J, N = 1024, 2048, 512, 512
FLOPS = 2 * 2 * K * N * J

F32 = mybir.dt.float32
BF16 = mybir.dt.bfloat16
I32 = mybir.dt.int32
U32 = mybir.dt.uint32
U16 = mybir.dt.uint16
U8 = mybir.dt.uint8
FP8X4 = mybir.dt.float8_e4m3fn_x4
FP4X4 = mybir.dt.float4_e2m1fn_x4
ACT = mybir.ActivationFunctionType
ALU = mybir.AluOpType

P = 128
PACK = 4
PASSES = K // (P * PACK)
CHUNK = 128
CHUNKS = J // CHUNK
LIST_COLS = CHUNK // 16
QUADS = 4
WB_ROW = 4


def tile_list_expert_contrast_pl_kernel(tc, xq, wa_words, wa_scales, wb_words, wb_scales, offs, out_0, out_1, out_2):
    nc = tc.nc
    with ExitStack() as ctx:
        keep = ctx.enter_context(tc.tile_pool(name="keep", bufs=1))
        psum = ctx.enter_context(tc.psum_pool(name="psum", bufs=1))

        offsets = keep.tile([P, J // 16], U16, name="offsets")
        wa_raw = [keep.tile([P, 2 * N], U8, name="wa_raw%d" % g, align_bytes=64) for g in range(PASSES)]
        wb_raw = [keep.tile([P, N], U32, name="wb_raw%d" % g, tag="wb_raw%d" % g, align_bytes=64) for g in range(PASSES)]
        scale_raw = keep.tile([P, PASSES * N], U8, name="scale_raw", align_bytes=64)
        xq_rows = xq.rearrange("(g p t) c -> g p t c", p=P, t=PACK)
        x_rows = {}

        def load_x(g, first, count):
            rows = keep.tile([P, count * T], F32, name="x_rows%d_%d" % (g, first))
            nc.sync.dma_start(out=rows[:].rearrange("p (t c) -> p t c", t=count), in_=xq_rows[g, :, first : first + count, :])
            for t in range(count):
                x_rows[g, first + t] = rows[:, t * T : (t + 1) * T]

        def load_wb(g):
            nc.sync.dma_start(out=wb_raw[g][:].bitcast(I32), in_=wb_words[g].rearrange("p n t -> p (n t)").bitcast(I32))

        def load_wa(g):
            nc.sync.dma_start(out=wa_raw[g][:].bitcast(I32), in_=wa_words[g].bitcast(I32))

        load_x(0, 0, 2)
        nc.sync.dma_start(offsets[:], offs)
        load_x(0, 2, 2)
        load_x(1, 0, 2)
        load_wb(1)
        load_wa(1)
        split_rows = keep.tile([P, T], F32, name="split_rows")
        x_rows[1, 2] = split_rows[:]
        nc.sync.dma_start(out=split_rows[:, : T // 2], in_=xq_rows[1, :, 2, : T // 2])
        load_wb(0)
        nc.sync.dma_start(out=split_rows[:, T // 2 :], in_=xq_rows[1, :, 2, T // 2 :])
        load_wa(0)
        load_x(1, 3, 1)

        nc.gpsimd.memset(scale_raw[:].bitcast(I32), 0)
        for scales, row in ((wb_scales, WB_ROW), (wa_scales, 0)):
            for quad in range(QUADS):
                first = 32 * quad + row
                nc.gpsimd.dma_start(
                    out=scale_raw[first : first + 4, :].bitcast(I32).rearrange("r (g n) -> r g n", g=PASSES),
                    in_=scales[:, 4 * quad : 4 * quad + 4, :].rearrange("g r n -> r g n").bitcast(I32),
                )


        x_codes = {}
        x_scale = {}

        def quantise_x(g, first, count, woven):
            codes = keep.tile([P, count * CHUNK], U32, name="x_codes%d_%d" % (g, first), align_bytes=64)
            scale = keep.tile([P, count * CHUNK], U8, name="x_scale%d_%d" % (g, first), align_bytes=64)
            nc.vector.quantize_mx(out=codes[:].bitcast(FP8X4), scales=scale[:], in_=woven.rearrange("p j t -> p (j t)"))
            for c in range(count):
                x_codes[g, first + c] = codes[:, c * CHUNK : (c + 1) * CHUNK]
                x_scale[g, first + c] = scale[:, c * CHUNK : (c + 1) * CHUNK]

        def listed(c, count):
            return offsets[:, c * LIST_COLS : (c + count) * LIST_COLS]

        wa_dealt = [keep.tile([P, 2 * N], U8, name="wa_dealt%d" % g, align_bytes=64) for g in range(PASSES)]
        wb_dealt = [keep.tile([P, N], U32, name="wb_dealt%d" % g, align_bytes=64) for g in range(PASSES)]

        def deal_wb(g):
            nc.vector.tensor_copy(
                out=wb_dealt[g][:].rearrange("p (t b i) -> p b t i", t=PACK, i=4),
                in_=wb_raw[g][:].rearrange("p (b i t) -> p b t i", t=PACK, i=4),
            )

        def deal_wa(g):
            nc.scalar.copy(
                out=wa_dealt[g][:].bitcast(U16).rearrange("p (t b i) -> p b t i", t=PACK, i=8),
                in_=wa_raw[g][:].bitcast(U16).rearrange("p (b i t) -> p b t i", t=PACK, i=8),
            )

        p_bank = [psum.tile([P, PACK * CHUNK], F32, name="p_bank%d" % c) for c in range(CHUNKS)]
        q_bank = [psum.tile([P, PACK * CHUNK], F32, name="q_bank%d" % c) for c in range(CHUNKS)]

        def multiply_q(g, c):
            for t in range(PACK):
                cols = slice(g * N + t * P, g * N + (t + 1) * P)
                nc.tensor.matmul_mx(
                    out=q_bank[c][:, t * CHUNK : (t + 1) * CHUNK],
                    lhsT=wb_dealt[g][:, t * P : (t + 1) * P].bitcast(FP8X4),
                    lhsT_scale=w_scale[WB_ROW:P, cols],
                    rhs=x_codes[g, c].bitcast(FP8X4),
                    rhs_scale=x_scale[g, c],
                    start=(g == 0 and t == 0),
                    stop=(g == PASSES - 1 and t == PACK - 1),
                )

        def multiply_p(g, c):
            for t in range(PACK):
                cols = slice(g * N + t * P, g * N + (t + 1) * P)
                nc.tensor.matmul_mx(
                    out=p_bank[c][:, t * CHUNK : (t + 1) * CHUNK],
                    lhsT=wa_dealt[g][:, t * 2 * P : (t + 1) * 2 * P].bitcast(FP4X4),
                    lhsT_scale=w_scale[:, cols],
                    rhs=x_codes[g, c].bitcast(FP8X4),
                    rhs_scale=x_scale[g, c],
                    start=(g == 0 and t == 0),
                    stop=(g == PASSES - 1 and t == PACK - 1),
                )

        HALF = CHUNKS // 2
        front_woven = [keep.tile([P, HALF * CHUNK, PACK], BF16, name="front_woven%d" % g, align_bytes=64) for g in range(PASSES)]
        back_picked = [keep.tile([P, PACK, HALF * CHUNK], F32, name="back_picked%d" % g) for g in range(PASSES)]
        back_woven = [keep.tile([P, HALF * CHUNK, PACK], BF16, name="back_woven%d" % g, align_bytes=64) for g in range(PASSES)]

        def gather(g, t):
            nc.vector.tensor_copy(out=front_woven[g][:, :, t], in_=x_rows[g, t].indirect(listed(0, HALF)))
            nc.scalar.activation(out=back_picked[g][:, t, :], in_=x_rows[g, t].indirect(listed(HALF, HALF)), func=ACT.Copy)

        def weave_back(g, rows):
            nc.scalar.copy(out=back_woven[g][:, :, rows], in_=back_picked[g][:, rows, :].rearrange("p t j -> p j t"))

        def quantise_pass(g):
            for c in range(HALF):
                quantise_x(g, c, 1, front_woven[g][:, c * CHUNK : (c + 1) * CHUNK, :])
            quantise_x(g, HALF, HALF, back_woven[g][:])

        for t in range(PACK):
            gather(0, t)
        weave_back(0, slice(0, PACK))
        quantise_pass(0)
        gather(1, 0)
        gather(1, 1)
        deal_wb(1)
        w_scale = keep.tile([P, PASSES * N], U8, name="w_scale", tag="wb_raw1", align_bytes=64)
        nc.vector.tensor_copy(
            out=w_scale[:].rearrange("p (g t b i) -> p g b t i", g=PASSES, t=PACK, i=16),
            in_=scale_raw[:].rearrange("p (g b i t) -> p g b t i", g=PASSES, t=PACK, i=16),
        )
        deal_wa(1)
        deal_wb(0)
        gather(1, 2)
        deal_wa(0)
        weave_back(1, slice(0, PACK - 1))
        for c in range(CHUNKS):
            multiply_q(0, c)
        for c in range(CHUNKS):
            multiply_p(0, c)
        gather(1, PACK - 1)
        weave_back(1, slice(PACK - 1, PACK))
        quantise_pass(1)

        multiply_q(PASSES - 1, 0)
        for c in range(CHUNKS):
            if c + 1 < CHUNKS:
                multiply_q(PASSES - 1, c + 1)
            multiply_p(PASSES - 1, c)

        y_rows = out_0.rearrange("(p t) j -> p t j", t=PACK)
        words = out_1[0].rearrange("p j t -> p (j t)").bitcast(I32)
        y_scale = keep.tile([P, J], U8, name="y_scale", align_bytes=64)
        q_sb = [keep.tile([P, PACK * CHUNK], F32, name="q_sb%d" % c) for c in range(CHUNKS)]
        diff = [keep.tile([P, PACK * CHUNK], F32, name="diff%d" % c, tag="diff%d" % c, align_bytes=64) for c in range(CHUNKS)]
        bent = [keep.tile([P, PACK * CHUNK], F32, name="bent%d" % c, tag="bent%d" % c, align_bytes=64) for c in range(CHUNKS)]
        y = [keep.tile([P, PACK, CHUNK], F32, name="y%d" % c) for c in range(CHUNKS)]
        last = CHUNKS - 1

        def fetch_q(c):
            nc.scalar.copy(out=q_sb[c][:], in_=q_bank[c][:])

        def subtract(c):
            nc.vector.tensor_tensor(out=diff[c][:], in0=p_bank[c][:], in1=q_sb[c][:], op=ALU.subtract)

        def bend(c):
            nc.scalar.activation(out=bent[c][:], in_=diff[c][:], func=ACT.Tanh)

        def add(c):
            nc.vector.tensor_tensor(out=y[c][:].rearrange("p t j -> p (t j)"), in0=p_bank[c][:], in1=bent[c][:], op=ALU.add)
            nc.sync.dma_start(out=y_rows[:, :, c * CHUNK : (c + 1) * CHUNK], in_=y[c][:])

        def quantise_y(woven_y, codes, first, count):
            cols = slice(first * CHUNK, (first + count) * CHUNK)
            nc.vector.quantize_mx(out=codes.bitcast(FP8X4), scales=y_scale[:, cols], in_=woven_y[:].rearrange("p j t -> p (j t)"))

        AHEAD = 2
        for step in range(CHUNKS + AHEAD):
            if step < CHUNKS:
                fetch_q(step)
                subtract(step)
            if step >= AHEAD:
                bend(step - AHEAD)
                add(step - AHEAD)
        front_y = keep.tile([P, HALF * CHUNK, PACK], BF16, name="front_y", tag="front_y", align_bytes=64)
        for c in range(HALF):
            nc.gpsimd.tensor_scalar(
                out=front_y[:, c * CHUNK : (c + 1) * CHUNK, :],
                in0=y[c][:].rearrange("p t j -> p j t"),
                scalar1=1.0,
                scalar2=0.0,
                op0=ALU.mult,
                op1=ALU.add,
            )
        front_codes = keep.tile([P, HALF * CHUNK], U32, name="front_codes", tag="bent%d" % last, align_bytes=64)
        quantise_y(front_y, front_codes[:], 0, HALF)
        nc.sync.dma_start(out=words[:, : HALF * CHUNK], in_=front_codes[:].bitcast(I32))
        back_codes = keep.tile([P, HALF * CHUNK], U32, name="back_codes", tag="front_y", align_bytes=64)
        for c in range(HALF, CHUNKS):
            back_y = keep.tile([P, CHUNK, PACK], BF16, name="back_y%d" % c, tag=("diff%d" % last if c == HALF else "back_y"), align_bytes=64)
            nc.scalar.copy(
                out=back_y[:].rearrange("p (b i) t -> p b t i", i=4),
                in_=y[c][:].rearrange("p t (b i) -> p b t i", i=4),
            )
            quantise_y(back_y, back_codes[:, (c - HALF) * CHUNK : (c - HALF + 1) * CHUNK], c, 1)
        nc.sync.dma_start(out=words[:, HALF * CHUNK :], in_=back_codes[:].bitcast(I32))
        for quad in range(QUADS):
            queue = nc.scalar if quad < 2 else nc.sync
            queue.dma_start(
                out=out_2[0, 4 * quad : 4 * quad + 4, :].bitcast(I32),
                in_=y_scale[32 * quad : 32 * quad + 4, :].bitcast(I32),
            )
